import numpy as np
import ml_dtypes

BF16 = ml_dtypes.bfloat16


def bf(x):
    return np.asarray(x, np.float32).astype(BF16)


def f32(x):
    return np.asarray(x, np.float32)


def f64(x):
    return np.asarray(x).astype(np.float64)


def striped(idx):
    return np.tile(idx.reshape(-1, 16).T, (8, 1))


S, K, M, N, D, V = 512, 128, 512, 192, 3, 64


def gelu_tanh(v):
    return 0.5 * v * (1.0 + np.tanh(np.sqrt(2.0 / np.pi) * (v + 0.044715 * v**3)))


def setup_inputs():
    return {"table": bf(np.random.standard_normal((K, S))), "w": bf(np.random.standard_normal((D, K, M)) / np.sqrt(D * K)), "b": f32(0.5 * np.random.standard_normal((M, 1))), "offs": striped(np.random.permutation(S)[:N])}


def reference(table, w, b, offs):
    idx = offs[:16].T.reshape(-1)
    x = f64(table)[:, idx]
    y = sum(f64(w)[t].T @ x[:, t * V : (t + 1) * V] for t in range(D))
    return gelu_tanh(y + f64(b))

@@ -1,0 +1,48 @@
+import concourse.mybir as mybir
+
+F32 = mybir.dt.float32
+BF16 = mybir.dt.bfloat16
+U16 = mybir.dt.uint16
+GELU_TANH = mybir.ActivationFunctionType.Gelu_apprx_tanh
+
+P = 128
+S = 512
+M = 512
+T = 3
+V = 64
+A = M // P
+PIECE = V // 16
+
+FLOPS = 2 * T * P * M * V
+
+
+def tile_gather_matmul_kernel(tc, table, w, b, offs, out):
+    nc = tc.nc
+    with (
+        tc.tile_pool(name="held", bufs=1) as held,
+        tc.psum_pool(name="psum", bufs=A) as psum,
+    ):
+        offsets = held.tile([P, T * PIECE], U16)
+        nodes = held.tile([P, S], BF16)
+        weights = held.tile([P, T, M], BF16)
+        bias = held.tile([P, A], F32)
+        result = held.tile([P, A, V], F32)
+
+        nc.sync.dma_start(offsets[:], offs)
+        nc.sync.dma_start(nodes[:], table)
+        nc.scalar.dma_start(weights[:], w.rearrange("t k m -> k t m"))
+        nc.scalar.dma_start(bias[:], b.rearrange("(p a) o -> p (a o)", a=A))
+
+        for a in range(A):
+            y = psum.tile([P, V], F32)
+            for t in range(T):
+                nc.tensor.matmul(
+                    y[:],
+                    weights[:, t, a::A],
+                    nodes[:].indirect(offsets[:, t * PIECE : (t + 1) * PIECE]),
+                    start=(t == 0),
+                    stop=(t == T - 1),
+                )
+            nc.scalar.activation(result[:, a, :], y[:], GELU_TANH, bias=bias[:, a : a + 1])
+
+        nc.sync.dma_start(out.rearrange("(p a) v -> p a v", a=A), result[:])

@@ -24,25 +24,32 @@ def tile_gather_matmul_kernel(tc, table, w, b, offs, out):
     ):
         offsets = held.tile([P, T * PIECE], U16)
         nodes = held.tile([P, S], BF16)
-        weights = held.tile([P, T, M], BF16)
+        weights = [held.tile([P, M], BF16, name=f"weights{t}") for t in range(T)]
         bias = held.tile([P, A], F32)
         result = held.tile([P, A, V], F32)
 
         nc.sync.dma_start(offsets[:], offs)
         nc.sync.dma_start(nodes[:], table)
-        nc.scalar.dma_start(weights[:], w.rearrange("t k m -> k t m"))
+        for t in range(T):
+            nc.scalar.dma_start(weights[t][:], w[t])
         nc.scalar.dma_start(bias[:], b.rearrange("(p a) o -> p (a o)", a=A))
 
-        for a in range(A):
-            y = psum.tile([P, V], F32)
-            for t in range(T):
+        zero = held.tile([P, 1], F32)
+        nc.vector.memset(zero[:], 0.0)
+        first_gelu = held.tile([P, 1], F32)
+        nc.scalar.activation(first_gelu[:], zero[:], GELU_TANH)
+
+        sums = [psum.tile([P, V], F32, name="sum") for a in range(A)]
+        for t in range(T):
+            for a in range(A):
                 nc.tensor.matmul(
-                    y[:],
-                    weights[:, t, a::A],
+                    sums[a][:],
+                    weights[t][:, a::A],
                     nodes[:].indirect(offsets[:, t * PIECE : (t + 1) * PIECE]),
                     start=(t == 0),
                     stop=(t == T - 1),
                 )
-            nc.scalar.activation(result[:, a, :], y[:], GELU_TANH, bias=bias[:, a : a + 1])
+        for a in range(A):
+            nc.scalar.activation(result[:, a, :], sums[a][:], GELU_TANH, bias=bias[:, a : a + 1])
 
         nc.sync.dma_start(out.rearrange("(p a) v -> p a v", a=A), result[:])

@@ -32,7 +32,7 @@ def tile_gather_matmul_kernel(tc, table, w, b, offs, out):
         nc.sync.dma_start(nodes[:], table)
         for t in range(T):
             nc.scalar.dma_start(weights[t][:], w[t])
-        nc.scalar.dma_start(bias[:], b.rearrange("(p a) o -> p (a o)", a=A))
+        nc.scalar.dma_start(bias[:], b.rearrange("(a p) o -> p (a o)", p=P))
 
         zero = held.tile([P, 1], F32)
         nc.vector.memset(zero[:], 0.0)
@@ -40,16 +40,21 @@ def tile_gather_matmul_kernel(tc, table, w, b, offs, out):
         nc.scalar.activation(first_gelu[:], zero[:], GELU_TANH)
 
         sums = [psum.tile([P, V], F32, name="sum") for a in range(A)]
-        for t in range(T):
-            for a in range(A):
-                nc.tensor.matmul(
-                    sums[a][:],
-                    weights[t][:, a::A],
-                    nodes[:].indirect(offsets[:, t * PIECE : (t + 1) * PIECE]),
-                    start=(t == 0),
-                    stop=(t == T - 1),
-                )
-        for a in range(A):
-            nc.scalar.activation(result[:, a, :], sums[a][:], GELU_TANH, bias=bias[:, a : a + 1])
+        def add_relation(t, a):
+            nc.tensor.matmul(
+                sums[a][:],
+                weights[t][:, a * P : (a + 1) * P],
+                nodes[:].indirect(offsets[:, t * PIECE : (t + 1) * PIECE]),
+                start=(t == 0),
+                stop=(t == T - 1),
+            )
 
-        nc.sync.dma_start(out.rearrange("(p a) v -> p a v", a=A), result[:])
+        out_rows = out.rearrange("(a p) v -> p a v", p=P)
+        for a in range(A):
+            add_relation(0, a)
+        for a in range(A):
+            for t in range(1, T):
+                add_relation(t, a)
+            nc.scalar.activation(result[:, a, :], sums[a][:], GELU_TANH, bias=bias[:, a : a + 1])
+            if a % 2 == 1:
+                nc.sync.dma_start(out_rows[:, a - 1 : a + 1, :], result[:, a - 1 : a + 1, :])

@@ -12,6 +12,7 @@ T = 3
 V = 64
 A = M // P
 PIECE = V // 16
+WARM = 4
 
 FLOPS = 2 * T * P * M * V
 
@@ -34,10 +35,13 @@ def tile_gather_matmul_kernel(tc, table, w, b, offs, out):
             nc.scalar.dma_start(weights[t][:], w[t])
         nc.scalar.dma_start(bias[:], b.rearrange("(a p) o -> p (a o)", p=P))
 
-        zero = held.tile([P, 1], F32)
-        nc.vector.memset(zero[:], 0.0)
+        zeros = held.tile([P, S], BF16)
+        nc.vector.memset(zeros[:], 0.0)
         first_gelu = held.tile([P, 1], F32)
-        nc.scalar.activation(first_gelu[:], zero[:], GELU_TANH)
+        nc.scalar.activation(first_gelu[:], zeros[:, :1], GELU_TANH)
+        warm = psum.tile([P, S], F32, bufs=1)
+        for i in range(WARM):
+            nc.tensor.matmul(warm[:], zeros[:, :P], zeros[:], start=True, stop=True)
 
         sums = [psum.tile([P, V], F32, name="sum") for a in range(A)]
         def add_relation(t, a):

import concourse.mybir as mybir

F32 = mybir.dt.float32
BF16 = mybir.dt.bfloat16
U16 = mybir.dt.uint16
GELU_TANH = mybir.ActivationFunctionType.Gelu_apprx_tanh

P = 128
S = 512
M = 512
T = 3
V = 64
A = M // P
PIECE = V // 16
WARM = 4

FLOPS = 2 * T * P * M * V


def tile_gather_matmul_kernel(tc, table, w, b, offs, out):
    nc = tc.nc
    with (
        tc.tile_pool(name="held", bufs=1) as held,
        tc.psum_pool(name="psum", bufs=A) as psum,
    ):
        offsets = held.tile([P, T * PIECE], U16)
        nodes = held.tile([P, S], BF16)
        weights = [held.tile([P, M], BF16, name=f"weights{t}") for t in range(T)]
        bias = held.tile([P, A], F32)
        result = held.tile([P, A, V], F32)

        nc.sync.dma_start(offsets[:], offs)
        nc.sync.dma_start(nodes[:], table)
        for t in range(T):
            nc.scalar.dma_start(weights[t][:], w[t])
        nc.scalar.dma_start(bias[:], b.rearrange("(a p) o -> p (a o)", p=P))

        zeros = held.tile([P, S], BF16)
        nc.vector.memset(zeros[:], 0.0)
        first_gelu = held.tile([P, 1], F32)
        nc.scalar.activation(first_gelu[:], zeros[:, :1], GELU_TANH)
        warm = psum.tile([P, S], F32, bufs=1)
        for i in range(WARM):
            nc.tensor.matmul(warm[:], zeros[:, :P], zeros[:], start=True, stop=True)

        sums = [psum.tile([P, V], F32, name="sum") for a in range(A)]
        def add_relation(t, a):
            nc.tensor.matmul(
                sums[a][:],
                weights[t][:, a * P : (a + 1) * P],
                nodes[:].indirect(offsets[:, t * PIECE : (t + 1) * PIECE]),
                start=(t == 0),
                stop=(t == T - 1),
            )

        out_rows = out.rearrange("(a p) v -> p a v", p=P)
        for a in range(A):
            add_relation(0, a)
        for a in range(A):
            for t in range(1, T):
                add_relation(t, a)
            nc.scalar.activation(result[:, a, :], sums[a][:], GELU_TANH, bias=bias[:, a : a + 1])
            if a % 2 == 1:
                nc.sync.dma_start(out_rows[:, a - 1 : a + 1, :], result[:, a - 1 : a + 1, :])
